import numpy as np
import ml_dtypes


def mxq(x, axis, fmt="e4m3"):
    dtype, down = {"e4m3": (ml_dtypes.float8_e4m3fn, 7), "e5m2": (ml_dtypes.float8_e5m2, 14)}[fmt]
    v = np.moveaxis(np.asarray(x, np.float32).astype(ml_dtypes.bfloat16).astype(np.float64), axis, -1)
    blocks = v.reshape(v.shape[:-1] + (-1, 32))
    amax = np.abs(blocks).max(-1, keepdims=True)
    byte = np.maximum(np.where(amax > 0, np.frexp(amax)[1] - 1 + 127, 0) - down, 1)
    scale = np.exp2(byte - 127.0)
    codes = (blocks / scale).astype(np.float32).astype(dtype).astype(np.float64)
    return np.moveaxis((codes * scale).reshape(v.shape), -1, axis)


WIDE = False


def mx_kscale(k):
    if not WIDE:
        return np.ones(k)
    levels = np.array([10, -10, 5, -5, 0])
    if k % 512:
        return np.exp2(np.random.permutation(np.resize(levels, k // 32))).repeat(32)
    a = np.empty((k // 512, 16))
    for p in range(k // 512):
        a[p, :8] = np.random.permutation(np.resize(levels, 8))
        for g in range(8):
            far = levels[np.abs(levels - a[p, g]) >= 10]
            a[p, g + 8] = far[np.random.randint(len(far))]
    return np.exp2(a.ravel()).repeat(32)


def f64(x):
    return np.asarray(x).astype(np.float64)


def striped(idx):
    return np.tile(idx.reshape(-1, 16).T, (8, 1)).astype(np.uint16)


def unstriped(offs):
    return offs[:16].T.reshape(-1).astype(np.int64)


def striped8(idx):
    return np.concatenate([x.reshape(-1, 16).T for x in idx]).astype(np.uint16)


def runs(offs, k):
    lists = np.stack([offs[16 * r : 16 * r + 16].T.reshape(-1) for r in range(8)]).astype(np.int64)
    return lists[np.arange(k) % 512 // 64]


def pack_weight(w):
    k, n = w.shape
    w = f64(np.asarray(w, np.float32).astype(ml_dtypes.bfloat16)).reshape(k // 32, 32, n)
    amax = np.abs(w).max(1)
    byte = np.clip(np.where(amax > 0, np.frexp(amax)[1] - 1 + 127 - 7, 1), 1, 254)
    scaled = (w * np.exp2(127.0 - byte)[:, None, :]).reshape(k, n).astype(np.float32)
    words = np.ascontiguousarray(scaled.reshape(k // 512, 128, 4, n).transpose(0, 1, 3, 2)).astype(ml_dtypes.float8_e4m3fn).view(np.uint8)
    return words, np.ascontiguousarray(byte.astype(np.uint8).reshape(k // 512, 16, n))


def unpack_weight(words, scales):
    g, p, n, _ = words.shape
    vals = np.ascontiguousarray(words).view(ml_dtypes.float8_e4m3fn).astype(np.float64) * np.repeat(np.exp2(scales.astype(np.float64) - 127.0), 8, axis=1)[..., None]
    return vals.transpose(0, 1, 3, 2).reshape(g * 512, n)


E2M1 = np.array([0.0, 0.5, 1.0, 1.5, 2.0, 3.0, 4.0, 6.0, -0.0, -0.5, -1.0, -1.5, -2.0, -3.0, -4.0, -6.0])


def pack_fp4(w):
    k, n = w.shape
    w = f64(np.asarray(w, np.float32).astype(ml_dtypes.bfloat16)).reshape(k // 32, 32, n)
    amax = np.abs(w).max(1)
    mant, ex = np.frexp(amax / 6.0)
    byte = np.clip(np.where(amax > 0, np.where(mant > 0.5, ex, ex - 1) + 127, 1), 1, 254)
    scaled = (w * np.exp2(127.0 - byte)[:, None, :]).reshape(k, n).astype(np.float32)
    c = np.ascontiguousarray(scaled.reshape(k // 512, 128, 4, n).transpose(0, 1, 3, 2)).astype(ml_dtypes.float4_e2m1fn).view(np.uint8) & 0xF
    words = (c[..., 0::2] | (c[..., 1::2] << 4)).reshape(k // 512, 128, 2 * n)
    return np.ascontiguousarray(words), np.ascontiguousarray(byte.astype(np.uint8).reshape(k // 512, 16, n))


def unpack_fp4(words, scales):
    g, _, n = scales.shape
    words = np.ascontiguousarray(words).reshape(g, 128, n, 2)
    nib = np.empty((g, 128, n, 4), np.uint8)
    nib[..., 0::2] = words & 0xF
    nib[..., 1::2] = words >> 4
    vals = E2M1[nib] * np.repeat(np.exp2(scales.astype(np.float64) - 127.0), 8, axis=1)[..., None]
    return vals.transpose(0, 1, 3, 2).reshape(g * 512, n)


def planes(y):
    n, m = y.shape
    v = y.astype(np.float32).astype(ml_dtypes.bfloat16).astype(np.float64).reshape(n // 32, 32, m)
    top = np.abs(v).max(1)
    byte = np.clip(np.where(top > 0, np.frexp(top)[1] - 1 + 127 - 7, 1), 1, 254)
    codes = (v * np.exp2(127.0 - byte)[:, None, :]).reshape(n, m).astype(np.float32).astype(ml_dtypes.float8_e4m3fn).view(np.uint8)
    words = codes.reshape(n // 512, 128, 4, m).transpose(0, 1, 3, 2)
    return np.ascontiguousarray(words), np.ascontiguousarray(byte.astype(np.uint8).reshape(n // 512, 16, m))


K, T, S, V, H, C = 512, 2048, 512, 256, 512, 512


def setup_inputs():
    n = np.random.standard_normal
    s = mx_kscale(K)[:, None]
    packed_xT = pack_weight(n((K, T)) * s)
    packed_w1 = pack_fp4(n((K, H)) / np.sqrt(K) / s)
    return {
        "x_words": packed_xT[0],
        "x_scales": packed_xT[1],
        "w1_words": packed_w1[0],
        "w1_scales": packed_w1[1],
        "gs": (np.random.uniform(0.5, 1.5, (K, 1)) / s).astype(np.float32),
        "wb": (n((K, V)) / np.sqrt(K) / s).astype(np.float32),
        "offs": striped(np.random.permutation(T)[:S]),
        "n1": striped8(np.stack([np.random.permutation(S) for _ in range(8)])),
        "cand": striped(np.random.permutation(T)[:C]),
        "cb": striped(np.random.permutation(T)[:C]),
        "n2": striped8(np.stack([np.random.permutation(V) for _ in range(8)])),
        "n3": striped8(np.stack([np.random.permutation(V) for _ in range(8)])),
    }


def reference(x_words, x_scales, w1_words, w1_scales, gs, wb, offs, n1, cand, cb, n2, n3):
    x_cand = unpack_weight(x_words, x_scales)[:, unstriped(cand)]
    xq = unpack_weight(x_words, x_scales)[:, unstriped(offs)]
    y = unpack_fp4(w1_words, w1_scales).T @ xq
    ln = y[np.arange(H)[:, None], runs(n1, H)]
    sq = (ln) ** 2
    ms = sq.reshape(H, V, 2).sum(axis=2)
    z = f64(gs) * np.sqrt(ms + 0.1)
    a = 0.0625 * ((x_cand.T @ mxq(z, 0, "e4m3")))
    x_cb = unpack_weight(x_words, x_scales)[:, unstriped(cb)]
    b = x_cb.T @ mxq(f64(wb), 0, "e4m3")
    out_0 = 0.75 * (a * (b[np.arange(C)[:, None], runs(n3, C)]) - ((a[np.arange(C)[:, None], runs(n2, C)]) * b))
    return (out_0,) + planes(out_0)

@@ -1,0 +1,224 @@
+from contextlib import ExitStack
+
+import concourse.mybir as mybir
+
+F32 = mybir.dt.float32
+BF16 = mybir.dt.bfloat16
+I32 = mybir.dt.int32
+U32 = mybir.dt.uint32
+U16 = mybir.dt.uint16
+U8 = mybir.dt.uint8
+FP8X4 = mybir.dt.float8_e4m3fn_x4
+FP4X4 = mybir.dt.float4_e2m1fn_x4
+ALU = mybir.AluOpType
+ACT = mybir.ActivationFunctionType
+
+P = 128
+PACK = 4
+T, S, V = 2048, 512, 256
+HALF = V // 2
+OUT_SCALE = 0.75 * 0.0625
+FLOPS = 2 * 512 * (512 * 512 + 2 * 512 * 256)
+
+
+def tile_picked_cdswcrossbhprms_none_po_kernel(
+    tc, x_words, x_scales, w1_words, w1_scales, gs, wb, offs, n1, cand, cb, n2, n3, out_0, out_1, out_2
+):
+    nc = tc.nc
+    with ExitStack() as ctx:
+        keep = ctx.enter_context(tc.tile_pool(name="keep", bufs=1))
+        psum = ctx.enter_context(tc.psum_pool(name="psum", bufs=1))
+
+        def sb(name, shape, dtype):
+            return keep.tile(shape, dtype, name=name, align_bytes=64)
+
+        def load_list(name, src):
+            tile = keep.tile([P, src.shape[1]], U16, name=name)
+            nc.sync.dma_start(tile[:], src)
+            return tile
+
+        def load_scale_rows(queue, tile, src):
+            rows = src[0].bitcast(I32)
+            for q in range(4):
+                queue.dma_start(out=tile[32 * q : 32 * q + 4, :].bitcast(I32), in_=rows[4 * q : 4 * q + 4, :])
+
+        xs = sb("xs", [P, T], U8)
+        w1s_raw = sb("w1s_raw", [P, S], U8)
+        nc.vector.memset(xs[:].bitcast(I32), 0)
+        nc.gpsimd.memset(w1s_raw[:].bitcast(I32), 0)
+
+        w1w_raw = sb("w1w_raw", [P, 2 * S], U8)
+        nc.sync.dma_start(out=w1w_raw[:].bitcast(I32), in_=w1_words[0].bitcast(I32))
+        offs_l = load_list("offs_l", offs)
+        load_scale_rows(nc.sync, xs, x_scales)
+        xw = sb("xw", [P, T], U32)
+        nc.sync.dma_start(out=xw[:].bitcast(I32), in_=x_words[0].rearrange("p n t -> p (n t)").bitcast(I32))
+        load_scale_rows(nc.scalar, w1s_raw, w1_scales)
+        cb_l = load_list("cb_l", cb)
+        n1_l = load_list("n1_l", n1)
+        wb_raw = sb("wb_raw", [P, PACK, V], F32)
+        nc.sync.dma_start(out=wb_raw[:], in_=wb.rearrange("(p j) v -> p j v", j=PACK))
+        cand_l = load_list("cand_l", cand)
+        gs_t = sb("gs_t", [P, PACK], F32)
+        nc.sync.dma_start(out=gs_t[:], in_=gs.rearrange("(p j) o -> p (j o)", j=PACK))
+        n3_l = load_list("n3_l", n3)
+        n2_l = load_list("n2_l", n2)
+
+        def pick(name, window, lst, dtype):
+            got = sb(name, [P, S], dtype)
+            nc.vector.tensor_copy(got[:], window[:].indirect(lst[:]))
+            return got
+
+        def deal(name, src, dtype, width):
+            dealt = sb(name, [P, S * width], dtype)
+            nc.vector.tensor_copy(
+                out=dealt[:].rearrange("p (t m b) -> p t m b", t=PACK, b=width),
+                in_=src[:].rearrange("p (m t b) -> p t m b", t=PACK, b=width),
+            )
+            return dealt
+
+        xq_s = pick("xq_s", xs, offs_l, U8)
+        w1w = deal("w1w", w1w_raw, U8, 2)
+        w1s = deal("w1s", w1s_raw, U8, 1)
+        xq_w = pick("xq_w", xw, offs_l, U32)
+
+        y_ps = [psum.tile([P, S], F32, name=f"y_ps{t}") for t in range(PACK)]
+        for t in range(PACK):
+            nc.tensor.matmul_mx(
+                out=y_ps[t][:],
+                lhsT=w1w[:, 2 * P * t : 2 * P * (t + 1)].bitcast(FP4X4),
+                lhsT_scale=w1s[:, P * t : P * (t + 1)],
+                rhs=xq_w[:].bitcast(FP8X4),
+                rhs_scale=xq_s[:],
+                start=True,
+                stop=True,
+            )
+
+        wb_bf = sb("wb_bf", [P, V, PACK], BF16)
+        nc.gpsimd.tensor_scalar(
+            out=wb_bf[:], in0=wb_raw[:].rearrange("p j v -> p v j"), scalar1=1.0, scalar2=0.0, op0=ALU.mult, op1=ALU.add
+        )
+        cb_w = deal("cb_w", pick("cb_w_raw", xw, cb_l, U32), U32, 1)
+        cb_s = deal("cb_s", pick("cb_s_raw", xs, cb_l, U8), U8, 1)
+        wb_w = sb("wb_w", [P, V], U32)
+        wb_s = sb("wb_s", [P, V], U8)
+        nc.vector.quantize_mx(out=wb_w[:].bitcast(FP8X4), scales=wb_s[:], in_=wb_bf[:].rearrange("p v j -> p (v j)"))
+        b_ps = [psum.tile([P, 2, V], F32, name=f"b_ps{u}") for u in range(2)]
+        for t in range(PACK):
+            nc.tensor.matmul_mx(
+                out=b_ps[t // 2][:, t % 2, :],
+                lhsT=cb_w[:, P * t : P * (t + 1)].bitcast(FP8X4),
+                lhsT_scale=cb_s[:, P * t : P * (t + 1)],
+                rhs=wb_w[:].bitcast(FP8X4),
+                rhs_scale=wb_s[:],
+                start=True,
+                stop=True,
+            )
+
+        ysq = [sb(f"ysq{t}", [P, S], F32) for t in range(PACK)]
+        sq = [sb(f"sq{h}", [P, PACK, V], F32) for h in range(2)]
+        ms = [sb(f"ms{h}", [P, PACK, HALF], F32) for h in range(2)]
+        root = [sb(f"root{h}", [P, HALF, PACK], F32) for h in range(2)]
+        z_bf = [sb(f"z_bf{h}", [P, HALF, PACK], BF16) for h in range(2)]
+        z_w = [sb(f"z_w{h}", [P, HALF], U32) for h in range(2)]
+        z_s = [sb(f"z_s{h}", [P, HALF], U8) for h in range(2)]
+        a_ps = [psum.tile([P, PACK, HALF], F32, name=f"a_ps{h}") for h in range(2)]
+        a_sb = [sb(f"a_sb{t}", [P, V], F32) for t in range(PACK)]
+        b_sb = [sb(f"b_sb{t}", [P, V], F32) for t in range(PACK)]
+        b_got = [sb(f"b_got{h}", [P, PACK, HALF], F32) for h in range(2)]
+        a_got = [sb(f"a_got{h}", [P, PACK, HALF], F32) for h in range(2)]
+        first = [sb(f"first{h}", [P, PACK, HALF], F32) for h in range(2)]
+        second = [sb(f"second{h}", [P, PACK, HALF], F32) for h in range(2)]
+        res = [sb(f"res{h}", [P, PACK, HALF], F32) for h in range(2)]
+        res_bf = [sb(f"res_bf{h}", [P, HALF, PACK], BF16) for h in range(2)]
+        res_w = sb("res_w", [P, V], U32)
+        res_s = sb("res_s", [P, V], U8)
+
+        def line_up(h, t):
+            nc.scalar.activation(sq[h][:, t, :], ysq[t][:].indirect(n1_l[:, 16 * h : 16 * (h + 1)]), ACT.Copy)
+
+        def pair_sum(h, t):
+            pairs = sq[h][:, t, :].rearrange("p (v e) -> p v e", e=2)
+            nc.vector.scalar_tensor_tensor(
+                out=ms[h][:, t, :], in0=pairs[:, :, 0], scalar=0.1, in1=pairs[:, :, 1], op0=ALU.add, op1=ALU.add
+            )
+
+        def finish_z(h):
+            nc.scalar.activation(root[h][:], ms[h][:].rearrange("p t v -> p v t"), ACT.Sqrt)
+            nc.vector.tensor_tensor(
+                out=z_bf[h][:], in0=root[h][:], in1=gs_t[:].unsqueeze(1).to_broadcast([P, HALF, PACK]), op=ALU.mult
+            )
+            nc.vector.quantize_mx(
+                out=z_w[h][:].bitcast(FP8X4), scales=z_s[h][:], in_=z_bf[h][:].rearrange("p v j -> p (v j)")
+            )
+
+        def score(h):
+            for t in range(PACK):
+                nc.tensor.matmul_mx(
+                    out=a_ps[h][:, t, :],
+                    lhsT=cand_w[:, P * t : P * (t + 1)].bitcast(FP8X4),
+                    lhsT_scale=cand_s[:, P * t : P * (t + 1)],
+                    rhs=z_w[h][:].bitcast(FP8X4),
+                    rhs_scale=z_s[h][:],
+                    start=True,
+                    stop=True,
+                )
+
+        def fetch(dst, windows, lst, h):
+            for t in range(PACK):
+                nc.scalar.activation(dst[h][:, t, :], windows[t][:].indirect(lst[:, 8 * h : 8 * (h + 1)]), ACT.Copy)
+
+        for t in range(PACK):
+            nc.scalar.activation(ysq[t][:], y_ps[t][:], ACT.Square)
+            line_up(0, t)
+        for t in range(PACK):
+            nc.vector.tensor_scalar(
+                out=b_sb[t][:], in0=b_ps[t // 2][:, t % 2, :], scalar1=OUT_SCALE, scalar2=None, op0=ALU.mult
+            )
+        for t in range(PACK):
+            pair_sum(0, t)
+        cand_w = deal("cand_w", pick("cand_w_raw", xw, cand_l, U32), U32, 1)
+        cand_s = deal("cand_s", pick("cand_s_raw", xs, cand_l, U8), U8, 1)
+        line_up(1, 0)
+        finish_z(0)
+        for t in range(1, PACK):
+            line_up(1, t)
+        for t in range(PACK):
+            pair_sum(1, t)
+        score(0)
+        fetch(b_got, b_sb, n3_l, 0)
+        finish_z(1)
+        score(1)
+        for t in range(PACK):
+            nc.vector.tensor_copy(out=a_sb[t][:, 0:HALF], in_=a_ps[0][:, t, :])
+        nc.vector.tensor_tensor(out=first[0][:], in0=a_ps[0][:], in1=b_got[0][:], op=ALU.mult)
+        fetch(b_got, b_sb, n3_l, 1)
+        for t in range(PACK):
+            nc.scalar.copy(out=a_sb[t][:, HALF:V], in_=a_ps[1][:, t, :])
+        nc.vector.tensor_tensor(out=first[1][:], in0=a_ps[1][:], in1=b_got[1][:], op=ALU.mult)
+
+        out_rows = out_0.rearrange("(p t) v -> p t v", t=PACK)
+        out_words = out_1[0].rearrange("p n t -> p (n t)").bitcast(I32)
+        for h in range(2):
+            cols = slice(HALF * h, HALF * (h + 1))
+            fetch(a_got, a_sb, n2_l, h)
+            for u in range(2):
+                nc.vector.scalar_tensor_tensor(
+                    out=second[h][:, 2 * u : 2 * u + 2, :],
+                    in0=b_ps[u][:, :, cols],
+                    scalar=OUT_SCALE,
+                    in1=a_got[h][:, 2 * u : 2 * u + 2, :],
+                    op0=ALU.mult,
+                    op1=ALU.mult,
+                )
+            nc.vector.tensor_tensor(out=res[h][:], in0=first[h][:], in1=second[h][:], op=ALU.subtract)
+            nc.sync.dma_start(out=out_rows[:, :, cols], in_=res[h][:])
+            nc.vector.tensor_copy(out=res_bf[h][:], in_=res[h][:].rearrange("p t v -> p v t"))
+            nc.vector.quantize_mx(
+                out=res_w[:, cols].bitcast(FP8X4), scales=res_s[:, cols], in_=res_bf[h][:].rearrange("p v j -> p (v j)")
+            )
+            nc.sync.dma_start(out=out_words[:, cols], in_=res_w[:, cols].bitcast(I32))
+        scale_rows = out_2[0].bitcast(I32)
+        for q in range(4):
+            queue = nc.scalar if q % 2 else nc.sync
+            queue.dma_start(out=scale_rows[4 * q : 4 * q + 4, :], in_=res_s[32 * q : 32 * q + 4, :].bitcast(I32))

@@ -1,6 +1,7 @@
 from contextlib import ExitStack
 
 import concourse.mybir as mybir
+from concourse.masks import make_identity
 
 F32 = mybir.dt.float32
 BF16 = mybir.dt.bfloat16
@@ -29,80 +30,99 @@ def tile_picked_cdswcrossbhprms_none_po_kernel(
         keep = ctx.enter_context(tc.tile_pool(name="keep", bufs=1))
         psum = ctx.enter_context(tc.psum_pool(name="psum", bufs=1))
 
-        def sb(name, shape, dtype):
-            return keep.tile(shape, dtype, name=name, align_bytes=64)
+        def sb(name, shape, dtype, tag=None):
+            return keep.tile(shape, dtype, name=name, tag=tag or name, align_bytes=64)
 
         def load_list(name, src):
             tile = keep.tile([P, src.shape[1]], U16, name=name)
             nc.sync.dma_start(tile[:], src)
             return tile
 
-        def load_scale_rows(queue, tile, src):
+        def load_scale_rows(queues, tile, src):
             rows = src[0].bitcast(I32)
             for q in range(4):
-                queue.dma_start(out=tile[32 * q : 32 * q + 4, :].bitcast(I32), in_=rows[4 * q : 4 * q + 4, :])
+                queues[q].dma_start(out=tile[32 * q : 32 * q + 4, :].bitcast(I32), in_=rows[4 * q : 4 * q + 4, :])
 
         xs = sb("xs", [P, T], U8)
         w1s_raw = sb("w1s_raw", [P, S], U8)
-        nc.vector.memset(xs[:].bitcast(I32), 0)
+        nc.vector.memset(xs[:, : T // 2].bitcast(I32), 0)
+        nc.gpsimd.memset(xs[:, T // 2 :].bitcast(I32), 0)
         nc.gpsimd.memset(w1s_raw[:].bitcast(I32), 0)
-
+        offs_l = load_list("offs_l", offs)
         w1w_raw = sb("w1w_raw", [P, 2 * S], U8)
         nc.sync.dma_start(out=w1w_raw[:].bitcast(I32), in_=w1_words[0].bitcast(I32))
-        offs_l = load_list("offs_l", offs)
-        load_scale_rows(nc.sync, xs, x_scales)
+        cb_l = load_list("cb_l", cb)
+        load_scale_rows([nc.sync, nc.sync, nc.scalar, nc.scalar], xs, x_scales)
         xw = sb("xw", [P, T], U32)
         nc.sync.dma_start(out=xw[:].bitcast(I32), in_=x_words[0].rearrange("p n t -> p (n t)").bitcast(I32))
-        load_scale_rows(nc.scalar, w1s_raw, w1_scales)
-        cb_l = load_list("cb_l", cb)
+        load_scale_rows([nc.sync] * 4, w1s_raw, w1_scales)
         n1_l = load_list("n1_l", n1)
+        cand_l = load_list("cand_l", cand)
         wb_raw = sb("wb_raw", [P, PACK, V], F32)
         nc.sync.dma_start(out=wb_raw[:], in_=wb.rearrange("(p j) v -> p j v", j=PACK))
-        cand_l = load_list("cand_l", cand)
         gs_t = sb("gs_t", [P, PACK], F32)
         nc.sync.dma_start(out=gs_t[:], in_=gs.rearrange("(p j) o -> p (j o)", j=PACK))
         n3_l = load_list("n3_l", n3)
         n2_l = load_list("n2_l", n2)
+        warm = sb("warm", [P, 1], F32)
+        nc.vector.memset(warm[:], 1.0)
+        warm_out = sb("warm_out", [P, 1], F32)
+        nc.scalar.activation(warm_out[:], warm[:], ACT.Sqrt)
+        ident = sb("ident", [P, P], F32)
+        make_identity(nc, ident[:])
 
-        def pick(name, window, lst, dtype):
-            got = sb(name, [P, S], dtype)
+        def pick(name, window, lst, dtype, tag=None):
+            got = sb(name, [P, S], dtype, tag)
             nc.vector.tensor_copy(got[:], window[:].indirect(lst[:]))
             return got
 
-        def deal(name, src, dtype, width):
+        def deal(name, src, dtype, width, engine=nc.vector):
             dealt = sb(name, [P, S * width], dtype)
-            nc.vector.tensor_copy(
+            engine.tensor_copy(
                 out=dealt[:].rearrange("p (t m b) -> p t m b", t=PACK, b=width),
                 in_=src[:].rearrange("p (m t b) -> p t m b", t=PACK, b=width),
             )
             return dealt
 
-        xq_s = pick("xq_s", xs, offs_l, U8)
         w1w = deal("w1w", w1w_raw, U8, 2)
-        w1s = deal("w1s", w1s_raw, U8, 1)
-        xq_w = pick("xq_w", xw, offs_l, U32)
+        xq_s = pick("xq_s", xs, offs_l, U8)
+        w1s = deal("w1s", w1s_raw, U8, 1, nc.gpsimd)
+        xq_w = sb("xq_w", [P, S], U32)
+        for h in range(2):
+            nc.vector.tensor_copy(xq_w[:, V * h : V * (h + 1)], xw[:].indirect(offs_l[:, 16 * h : 16 * (h + 1)]))
 
-        y_ps = [psum.tile([P, S], F32, name=f"y_ps{t}") for t in range(PACK)]
-        for t in range(PACK):
+        y_ps = [psum.tile([P, S], F32, name=f"y_ps{t}", tag=f"bank{t}") for t in range(PACK)]
+        ysq = [sb(f"ysq{t}", [P, S], F32) for t in range(PACK)]
+
+        def project(t, cols):
             nc.tensor.matmul_mx(
-                out=y_ps[t][:],
+                out=y_ps[t][:, cols],
                 lhsT=w1w[:, 2 * P * t : 2 * P * (t + 1)].bitcast(FP4X4),
                 lhsT_scale=w1s[:, P * t : P * (t + 1)],
-                rhs=xq_w[:].bitcast(FP8X4),
-                rhs_scale=xq_s[:],
+                rhs=xq_w[:, cols].bitcast(FP8X4),
+                rhs_scale=xq_s[:, cols],
                 start=True,
                 stop=True,
             )
+
+        for h in range(2):
+            cols = slice(V * h, V * (h + 1))
+            project(0, cols)
+            nc.scalar.activation(ysq[0][:, cols], y_ps[0][:, cols], ACT.Square)
+        for t in range(1, PACK):
+            project(t, slice(0, S))
 
         wb_bf = sb("wb_bf", [P, V, PACK], BF16)
         nc.gpsimd.tensor_scalar(
             out=wb_bf[:], in0=wb_raw[:].rearrange("p j v -> p v j"), scalar1=1.0, scalar2=0.0, op0=ALU.mult, op1=ALU.add
         )
         cb_w = deal("cb_w", pick("cb_w_raw", xw, cb_l, U32), U32, 1)
-        cb_s = deal("cb_s", pick("cb_s_raw", xs, cb_l, U8), U8, 1)
+        cb_s = deal("cb_s", pick("cb_s_raw", xs, cb_l, U8, "w1s_raw"), U8, 1)
         wb_w = sb("wb_w", [P, V], U32)
         wb_s = sb("wb_s", [P, V], U8)
         nc.vector.quantize_mx(out=wb_w[:].bitcast(FP8X4), scales=wb_s[:], in_=wb_bf[:].rearrange("p v j -> p (v j)"))
+        cand_w = deal("cand_w", pick("cand_w_raw", xw, cand_l, U32, "wb_bf"), U32, 1)
+        cand_s = deal("cand_s", pick("cand_s_raw", xs, cand_l, U8, "wb_bf"), U8, 1)
         b_ps = [psum.tile([P, 2, V], F32, name=f"b_ps{u}") for u in range(2)]
         for t in range(PACK):
             nc.tensor.matmul_mx(
@@ -115,19 +135,16 @@ def tile_picked_cdswcrossbhprms_none_po_kernel(
                 stop=True,
             )
 
-        ysq = [sb(f"ysq{t}", [P, S], F32) for t in range(PACK)]
         sq = [sb(f"sq{h}", [P, PACK, V], F32) for h in range(2)]
-        ms = [sb(f"ms{h}", [P, PACK, HALF], F32) for h in range(2)]
-        root = [sb(f"root{h}", [P, HALF, PACK], F32) for h in range(2)]
+        root = [sb(f"root{h}", [P, PACK, P], F32) for h in range(2)]
+        ms_ps = {}
         z_bf = [sb(f"z_bf{h}", [P, HALF, PACK], BF16) for h in range(2)]
         z_w = [sb(f"z_w{h}", [P, HALF], U32) for h in range(2)]
         z_s = [sb(f"z_s{h}", [P, HALF], U8) for h in range(2)]
         a_ps = [psum.tile([P, PACK, HALF], F32, name=f"a_ps{h}") for h in range(2)]
         a_sb = [sb(f"a_sb{t}", [P, V], F32) for t in range(PACK)]
         b_sb = [sb(f"b_sb{t}", [P, V], F32) for t in range(PACK)]
-        b_got = [sb(f"b_got{h}", [P, PACK, HALF], F32) for h in range(2)]
         a_got = [sb(f"a_got{h}", [P, PACK, HALF], F32) for h in range(2)]
-        first = [sb(f"first{h}", [P, PACK, HALF], F32) for h in range(2)]
         second = [sb(f"second{h}", [P, PACK, HALF], F32) for h in range(2)]
         res = [sb(f"res{h}", [P, PACK, HALF], F32) for h in range(2)]
         res_bf = [sb(f"res_bf{h}", [P, HALF, PACK], BF16) for h in range(2)]
@@ -138,15 +155,24 @@ def tile_picked_cdswcrossbhprms_none_po_kernel(
             nc.scalar.activation(sq[h][:, t, :], ysq[t][:].indirect(n1_l[:, 16 * h : 16 * (h + 1)]), ACT.Copy)
 
         def pair_sum(h, t):
+            if t == 0:
+                ms_ps[h] = psum.tile([P, PACK, P], F32, name=f"ms_ps{h}", tag=f"bank{2 * h}")
             pairs = sq[h][:, t, :].rearrange("p (v e) -> p v e", e=2)
-            nc.vector.scalar_tensor_tensor(
-                out=ms[h][:, t, :], in0=pairs[:, :, 0], scalar=0.1, in1=pairs[:, :, 1], op0=ALU.add, op1=ALU.add
-            )
+            for e in range(2):
+                nc.tensor.matmul(
+                    ms_ps[h][:, t, :], pairs[:, :, e], ident[:], is_transpose=True, start=(e == 0), stop=(e == 1)
+                )
 
         def finish_z(h):
-            nc.scalar.activation(root[h][:], ms[h][:].rearrange("p t v -> p v t"), ACT.Sqrt)
+            nc.scalar.activation(root[h][:], ms_ps[h][:], ACT.Sqrt, bias=0.1)
+            root_ps = psum.tile([P, PACK, HALF], F32, name=f"root_ps{h}", tag=f"bank{2 * h + 1}")
+            for t in range(PACK):
+                nc.tensor.transpose(root_ps[:, t, :], root[h][:, t, :], ident[:])
             nc.vector.tensor_tensor(
-                out=z_bf[h][:], in0=root[h][:], in1=gs_t[:].unsqueeze(1).to_broadcast([P, HALF, PACK]), op=ALU.mult
+                out=z_bf[h][:],
+                in0=root_ps[:].rearrange("p t v -> p v t"),
+                in1=gs_t[:].unsqueeze(1).to_broadcast([P, HALF, PACK]),
+                op=ALU.mult,
             )
             nc.vector.quantize_mx(
                 out=z_w[h][:].bitcast(FP8X4), scales=z_s[h][:], in_=z_bf[h][:].rearrange("p v j -> p (v j)")
@@ -168,17 +194,16 @@ def tile_picked_cdswcrossbhprms_none_po_kernel(
             for t in range(PACK):
                 nc.scalar.activation(dst[h][:, t, :], windows[t][:].indirect(lst[:, 8 * h : 8 * (h + 1)]), ACT.Copy)
 
-        for t in range(PACK):
+        line_up(0, 0)
+        for t in range(1, PACK):
             nc.scalar.activation(ysq[t][:], y_ps[t][:], ACT.Square)
             line_up(0, t)
+        for t in range(PACK):
+            pair_sum(0, t)
         for t in range(PACK):
             nc.vector.tensor_scalar(
                 out=b_sb[t][:], in0=b_ps[t // 2][:, t % 2, :], scalar1=OUT_SCALE, scalar2=None, op0=ALU.mult
             )
-        for t in range(PACK):
-            pair_sum(0, t)
-        cand_w = deal("cand_w", pick("cand_w_raw", xw, cand_l, U32), U32, 1)
-        cand_s = deal("cand_s", pick("cand_s_raw", xs, cand_l, U8), U8, 1)
         line_up(1, 0)
         finish_z(0)
         for t in range(1, PACK):
@@ -186,22 +211,26 @@ def tile_picked_cdswcrossbhprms_none_po_kernel(
         for t in range(PACK):
             pair_sum(1, t)
         score(0)
-        fetch(b_got, b_sb, n3_l, 0)
         finish_z(1)
+        b_got_all = sb("b_got", [P, 2, PACK, HALF], F32, "sq1")
+        b_got = [b_got_all[:, h] for h in range(2)]
+        fetch(b_got, b_sb, n3_l, 0)
         score(1)
+        first = [sb("first0", [P, PACK, HALF], F32, "z_bf1"), sb("first1", [P, PACK, HALF], F32)]
         for t in range(PACK):
             nc.vector.tensor_copy(out=a_sb[t][:, 0:HALF], in_=a_ps[0][:, t, :])
-        nc.vector.tensor_tensor(out=first[0][:], in0=a_ps[0][:], in1=b_got[0][:], op=ALU.mult)
+        nc.vector.tensor_tensor(out=first[0][:], in0=a_ps[0][:], in1=b_got[0], op=ALU.mult)
         fetch(b_got, b_sb, n3_l, 1)
         for t in range(PACK):
-            nc.scalar.copy(out=a_sb[t][:, HALF:V], in_=a_ps[1][:, t, :])
-        nc.vector.tensor_tensor(out=first[1][:], in0=a_ps[1][:], in1=b_got[1][:], op=ALU.mult)
+            nc.vector.tensor_copy(out=a_sb[t][:, HALF:V], in_=a_ps[1][:, t, :])
+        nc.vector.tensor_tensor(out=first[1][:], in0=a_ps[1][:], in1=b_got[1], op=ALU.mult)
 
         out_rows = out_0.rearrange("(p t) v -> p t v", t=PACK)
         out_words = out_1[0].rearrange("p n t -> p (n t)").bitcast(I32)
         for h in range(2):
-            cols = slice(HALF * h, HALF * (h + 1))
             fetch(a_got, a_sb, n2_l, h)
+        for h in range(2):
+            cols = slice(HALF * h, HALF * (h + 1))
             for u in range(2):
                 nc.vector.scalar_tensor_tensor(
                     out=second[h][:, 2 * u : 2 * u + 2, :],
@@ -211,9 +240,16 @@ def tile_picked_cdswcrossbhprms_none_po_kernel(
                     op0=ALU.mult,
                     op1=ALU.mult,
                 )
-            nc.vector.tensor_tensor(out=res[h][:], in0=first[h][:], in1=second[h][:], op=ALU.subtract)
+            for u in range(2):
+                two = slice(2 * u, 2 * u + 2)
+                nc.vector.tensor_tensor(
+                    out=res[h][:, two, :], in0=first[h][:, two, :], in1=second[h][:, two, :], op=ALU.subtract
+                )
             nc.sync.dma_start(out=out_rows[:, :, cols], in_=res[h][:])
-            nc.vector.tensor_copy(out=res_bf[h][:], in_=res[h][:].rearrange("p t v -> p v t"))
+        nc.scalar.copy(out=res_bf[0][:], in_=res[0][:].rearrange("p t v -> p v t"))
+        nc.vector.tensor_copy(out=res_bf[1][:], in_=res[1][:].rearrange("p t v -> p v t"))
+        for h in range(2):
+            cols = slice(HALF * h, HALF * (h + 1))
             nc.vector.quantize_mx(
                 out=res_w[:, cols].bitcast(FP8X4), scales=res_s[:, cols], in_=res_bf[h][:].rearrange("p v j -> p (v j)")
             )

@@ -135,13 +135,12 @@ def tile_picked_cdswcrossbhprms_none_po_kernel(
                 stop=True,
             )
 
-        sq = [sb(f"sq{h}", [P, PACK, V], F32) for h in range(2)]
+        sq = {}
         root = [sb(f"root{h}", [P, PACK, P], F32) for h in range(2)]
-        ms_ps = {}
         z_bf = [sb(f"z_bf{h}", [P, HALF, PACK], BF16) for h in range(2)]
         z_w = [sb(f"z_w{h}", [P, HALF], U32) for h in range(2)]
         z_s = [sb(f"z_s{h}", [P, HALF], U8) for h in range(2)]
-        a_ps = [psum.tile([P, PACK, HALF], F32, name=f"a_ps{h}") for h in range(2)]
+        a_first = psum.tile([P, PACK, HALF], F32, name="a_first")
         a_sb = [sb(f"a_sb{t}", [P, V], F32) for t in range(PACK)]
         b_sb = [sb(f"b_sb{t}", [P, V], F32) for t in range(PACK)]
         a_got = [sb(f"a_got{h}", [P, PACK, HALF], F32) for h in range(2)]
@@ -152,22 +151,25 @@ def tile_picked_cdswcrossbhprms_none_po_kernel(
         res_s = sb("res_s", [P, V], U8)
 
         def line_up(h, t):
-            nc.scalar.activation(sq[h][:, t, :], ysq[t][:].indirect(n1_l[:, 16 * h : 16 * (h + 1)]), ACT.Copy)
+            nc.scalar.activation(sq[h, t], ysq[t][:].indirect(n1_l[:, 16 * h : 16 * (h + 1)]), ACT.Copy)
 
-        def pair_sum(h, t):
-            if t == 0:
-                ms_ps[h] = psum.tile([P, PACK, P], F32, name=f"ms_ps{h}", tag=f"bank{2 * h}")
-            pairs = sq[h][:, t, :].rearrange("p (v e) -> p v e", e=2)
+        def pair_sum(h, t, dst):
+            pairs = sq[h, t].rearrange("p (v e) -> p v e", e=2)
             for e in range(2):
-                nc.tensor.matmul(
-                    ms_ps[h][:, t, :], pairs[:, :, e], ident[:], is_transpose=True, start=(e == 0), stop=(e == 1)
-                )
+                nc.tensor.matmul(dst, pairs[:, :, e], ident[:], is_transpose=True, start=(e == 0), stop=(e == 1))
 
-        def finish_z(h):
-            nc.scalar.activation(root[h][:], ms_ps[h][:], ACT.Sqrt, bias=0.1)
+        def pair_sums(h, tiles, bank):
+            ms_ps = psum.tile([P, len(tiles), P], F32, name=f"ms_ps{h}_{tiles[0]}", tag=bank)
+            for i, t in enumerate(tiles):
+                pair_sum(h, t, ms_ps[:, i, :])
+            return tiles, ms_ps
+
+        def finish_z(h, sums):
             root_ps = psum.tile([P, PACK, HALF], F32, name=f"root_ps{h}", tag=f"bank{2 * h + 1}")
-            for t in range(PACK):
-                nc.tensor.transpose(root_ps[:, t, :], root[h][:, t, :], ident[:])
+            for tiles, ms_ps in sums:
+                nc.scalar.activation(root[h][:, tiles[0] : tiles[-1] + 1, :], ms_ps[:], ACT.Sqrt, bias=0.1)
+                for t in tiles:
+                    nc.tensor.transpose(root_ps[:, t, :], root[h][:, t, :], ident[:])
             nc.vector.tensor_tensor(
                 out=z_bf[h][:],
                 in0=root_ps[:].rearrange("p t v -> p v t"),
@@ -178,10 +180,10 @@ def tile_picked_cdswcrossbhprms_none_po_kernel(
                 out=z_w[h][:].bitcast(FP8X4), scales=z_s[h][:], in_=z_bf[h][:].rearrange("p v j -> p (v j)")
             )
 
-        def score(h):
+        def score(h, dst):
             for t in range(PACK):
                 nc.tensor.matmul_mx(
-                    out=a_ps[h][:, t, :],
+                    out=dst[t],
                     lhsT=cand_w[:, P * t : P * (t + 1)].bitcast(FP8X4),
                     lhsT_scale=cand_s[:, P * t : P * (t + 1)],
                     rhs=z_w[h][:].bitcast(FP8X4),
@@ -194,36 +196,45 @@ def tile_picked_cdswcrossbhprms_none_po_kernel(
             for t in range(PACK):
                 nc.scalar.activation(dst[h][:, t, :], windows[t][:].indirect(lst[:, 8 * h : 8 * (h + 1)]), ACT.Copy)
 
+        sq_first = sb("sq_first", [P, PACK, V], F32)
+        sq_mid = sb("sq_mid", [P, 2, V], F32)
+        for t in range(PACK):
+            sq[0, t] = sq_first[:, t, :]
+        for t in range(2):
+            sq[1, t] = sq_mid[:, t, :]
         line_up(0, 0)
         for t in range(1, PACK):
             nc.scalar.activation(ysq[t][:], y_ps[t][:], ACT.Square)
             line_up(0, t)
-        for t in range(PACK):
-            pair_sum(0, t)
+        sums_first = [pair_sums(0, [0, 1, 2, 3], "bank0")]
         for t in range(PACK):
             nc.vector.tensor_scalar(
                 out=b_sb[t][:], in0=b_ps[t // 2][:, t % 2, :], scalar1=OUT_SCALE, scalar2=None, op0=ALU.mult
             )
         line_up(1, 0)
-        finish_z(0)
-        for t in range(1, PACK):
+        line_up(1, 1)
+        finish_z(0, sums_first)
+        sq_last = sb("sq_last", [P, 2, V], F32, "sq_first")
+        for t in range(2, PACK):
+            sq[1, t] = sq_last[:, t - 2, :]
             line_up(1, t)
-        for t in range(PACK):
-            pair_sum(1, t)
-        score(0)
-        finish_z(1)
-        b_got_all = sb("b_got", [P, 2, PACK, HALF], F32, "sq1")
+        sums_last = [pair_sums(1, [0, 1, 2], "bank2"), pair_sums(1, [3], "bank4")]
+        score(0, [a_first[:, t, :] for t in range(PACK)])
+        finish_z(1, sums_last)
+        b_got_all = sb("b_got", [P, 2, PACK, HALF], F32, "sq_first")
         b_got = [b_got_all[:, h] for h in range(2)]
         fetch(b_got, b_sb, n3_l, 0)
-        score(1)
+        a_last = [psum.tile([P, HALF], F32, name=f"a_last{t}", tag=f"bank{t}") for t in range(PACK)]
+        score(1, [tile[:] for tile in a_last])
         first = [sb("first0", [P, PACK, HALF], F32, "z_bf1"), sb("first1", [P, PACK, HALF], F32)]
         for t in range(PACK):
-            nc.vector.tensor_copy(out=a_sb[t][:, 0:HALF], in_=a_ps[0][:, t, :])
-        nc.vector.tensor_tensor(out=first[0][:], in0=a_ps[0][:], in1=b_got[0], op=ALU.mult)
+            nc.vector.tensor_copy(out=a_sb[t][:, 0:HALF], in_=a_first[:, t, :])
+        nc.vector.tensor_tensor(out=first[0][:], in0=a_first[:], in1=b_got[0], op=ALU.mult)
         fetch(b_got, b_sb, n3_l, 1)
         for t in range(PACK):
-            nc.vector.tensor_copy(out=a_sb[t][:, HALF:V], in_=a_ps[1][:, t, :])
-        nc.vector.tensor_tensor(out=first[1][:], in0=a_ps[1][:], in1=b_got[1], op=ALU.mult)
+            nc.vector.tensor_copy(out=a_sb[t][:, HALF:V], in_=a_last[t][:])
+        for t in range(PACK):
+            nc.vector.tensor_tensor(out=first[1][:, t, :], in0=a_last[t][:], in1=b_got[1][:, t, :], op=ALU.mult)
 
         out_rows = out_0.rearrange("(p t) v -> p t v", t=PACK)
         out_words = out_1[0].rearrange("p n t -> p (n t)").bitcast(I32)

from contextlib import ExitStack

import concourse.mybir as mybir
from concourse.masks import make_identity

F32 = mybir.dt.float32
BF16 = mybir.dt.bfloat16
I32 = mybir.dt.int32
U32 = mybir.dt.uint32
U16 = mybir.dt.uint16
U8 = mybir.dt.uint8
FP8X4 = mybir.dt.float8_e4m3fn_x4
FP4X4 = mybir.dt.float4_e2m1fn_x4
ALU = mybir.AluOpType
ACT = mybir.ActivationFunctionType

P = 128
PACK = 4
T, S, V = 2048, 512, 256
HALF = V // 2
OUT_SCALE = 0.75 * 0.0625
FLOPS = 2 * 512 * (512 * 512 + 2 * 512 * 256)


def tile_picked_cdswcrossbhprms_none_po_kernel(
    tc, x_words, x_scales, w1_words, w1_scales, gs, wb, offs, n1, cand, cb, n2, n3, out_0, out_1, out_2
):
    nc = tc.nc
    with ExitStack() as ctx:
        keep = ctx.enter_context(tc.tile_pool(name="keep", bufs=1))
        psum = ctx.enter_context(tc.psum_pool(name="psum", bufs=1))

        def sb(name, shape, dtype, tag=None):
            return keep.tile(shape, dtype, name=name, tag=tag or name, align_bytes=64)

        def load_list(name, src):
            tile = keep.tile([P, src.shape[1]], U16, name=name)
            nc.sync.dma_start(tile[:], src)
            return tile

        def load_scale_rows(queues, tile, src):
            rows = src[0].bitcast(I32)
            for q in range(4):
                queues[q].dma_start(out=tile[32 * q : 32 * q + 4, :].bitcast(I32), in_=rows[4 * q : 4 * q + 4, :])

        xs = sb("xs", [P, T], U8)
        w1s_raw = sb("w1s_raw", [P, S], U8)
        nc.vector.memset(xs[:, : T // 2].bitcast(I32), 0)
        nc.gpsimd.memset(xs[:, T // 2 :].bitcast(I32), 0)
        nc.gpsimd.memset(w1s_raw[:].bitcast(I32), 0)
        offs_l = load_list("offs_l", offs)
        w1w_raw = sb("w1w_raw", [P, 2 * S], U8)
        nc.sync.dma_start(out=w1w_raw[:].bitcast(I32), in_=w1_words[0].bitcast(I32))
        cb_l = load_list("cb_l", cb)
        load_scale_rows([nc.sync, nc.sync, nc.scalar, nc.scalar], xs, x_scales)
        xw = sb("xw", [P, T], U32)
        nc.sync.dma_start(out=xw[:].bitcast(I32), in_=x_words[0].rearrange("p n t -> p (n t)").bitcast(I32))
        load_scale_rows([nc.sync] * 4, w1s_raw, w1_scales)
        n1_l = load_list("n1_l", n1)
        cand_l = load_list("cand_l", cand)
        wb_raw = sb("wb_raw", [P, PACK, V], F32)
        nc.sync.dma_start(out=wb_raw[:], in_=wb.rearrange("(p j) v -> p j v", j=PACK))
        gs_t = sb("gs_t", [P, PACK], F32)
        nc.sync.dma_start(out=gs_t[:], in_=gs.rearrange("(p j) o -> p (j o)", j=PACK))
        n3_l = load_list("n3_l", n3)
        n2_l = load_list("n2_l", n2)
        warm = sb("warm", [P, 1], F32)
        nc.vector.memset(warm[:], 1.0)
        warm_out = sb("warm_out", [P, 1], F32)
        nc.scalar.activation(warm_out[:], warm[:], ACT.Sqrt)
        ident = sb("ident", [P, P], F32)
        make_identity(nc, ident[:])

        def pick(name, window, lst, dtype, tag=None):
            got = sb(name, [P, S], dtype, tag)
            nc.vector.tensor_copy(got[:], window[:].indirect(lst[:]))
            return got

        def deal(name, src, dtype, width, engine=nc.vector):
            dealt = sb(name, [P, S * width], dtype)
            engine.tensor_copy(
                out=dealt[:].rearrange("p (t m b) -> p t m b", t=PACK, b=width),
                in_=src[:].rearrange("p (m t b) -> p t m b", t=PACK, b=width),
            )
            return dealt

        w1w = deal("w1w", w1w_raw, U8, 2)
        xq_s = pick("xq_s", xs, offs_l, U8)
        w1s = deal("w1s", w1s_raw, U8, 1, nc.gpsimd)
        xq_w = sb("xq_w", [P, S], U32)
        for h in range(2):
            nc.vector.tensor_copy(xq_w[:, V * h : V * (h + 1)], xw[:].indirect(offs_l[:, 16 * h : 16 * (h + 1)]))

        y_ps = [psum.tile([P, S], F32, name=f"y_ps{t}", tag=f"bank{t}") for t in range(PACK)]
        ysq = [sb(f"ysq{t}", [P, S], F32) for t in range(PACK)]

        def project(t, cols):
            nc.tensor.matmul_mx(
                out=y_ps[t][:, cols],
                lhsT=w1w[:, 2 * P * t : 2 * P * (t + 1)].bitcast(FP4X4),
                lhsT_scale=w1s[:, P * t : P * (t + 1)],
                rhs=xq_w[:, cols].bitcast(FP8X4),
                rhs_scale=xq_s[:, cols],
                start=True,
                stop=True,
            )

        for h in range(2):
            cols = slice(V * h, V * (h + 1))
            project(0, cols)
            nc.scalar.activation(ysq[0][:, cols], y_ps[0][:, cols], ACT.Square)
        for t in range(1, PACK):
            project(t, slice(0, S))

        wb_bf = sb("wb_bf", [P, V, PACK], BF16)
        nc.gpsimd.tensor_scalar(
            out=wb_bf[:], in0=wb_raw[:].rearrange("p j v -> p v j"), scalar1=1.0, scalar2=0.0, op0=ALU.mult, op1=ALU.add
        )
        cb_w = deal("cb_w", pick("cb_w_raw", xw, cb_l, U32), U32, 1)
        cb_s = deal("cb_s", pick("cb_s_raw", xs, cb_l, U8, "w1s_raw"), U8, 1)
        wb_w = sb("wb_w", [P, V], U32)
        wb_s = sb("wb_s", [P, V], U8)
        nc.vector.quantize_mx(out=wb_w[:].bitcast(FP8X4), scales=wb_s[:], in_=wb_bf[:].rearrange("p v j -> p (v j)"))
        cand_w = deal("cand_w", pick("cand_w_raw", xw, cand_l, U32, "wb_bf"), U32, 1)
        cand_s = deal("cand_s", pick("cand_s_raw", xs, cand_l, U8, "wb_bf"), U8, 1)
        b_ps = [psum.tile([P, 2, V], F32, name=f"b_ps{u}") for u in range(2)]
        for t in range(PACK):
            nc.tensor.matmul_mx(
                out=b_ps[t // 2][:, t % 2, :],
                lhsT=cb_w[:, P * t : P * (t + 1)].bitcast(FP8X4),
                lhsT_scale=cb_s[:, P * t : P * (t + 1)],
                rhs=wb_w[:].bitcast(FP8X4),
                rhs_scale=wb_s[:],
                start=True,
                stop=True,
            )

        sq = {}
        root = [sb(f"root{h}", [P, PACK, P], F32) for h in range(2)]
        z_bf = [sb(f"z_bf{h}", [P, HALF, PACK], BF16) for h in range(2)]
        z_w = [sb(f"z_w{h}", [P, HALF], U32) for h in range(2)]
        z_s = [sb(f"z_s{h}", [P, HALF], U8) for h in range(2)]
        a_first = psum.tile([P, PACK, HALF], F32, name="a_first")
        a_sb = [sb(f"a_sb{t}", [P, V], F32) for t in range(PACK)]
        b_sb = [sb(f"b_sb{t}", [P, V], F32) for t in range(PACK)]
        a_got = [sb(f"a_got{h}", [P, PACK, HALF], F32) for h in range(2)]
        second = [sb(f"second{h}", [P, PACK, HALF], F32) for h in range(2)]
        res = [sb(f"res{h}", [P, PACK, HALF], F32) for h in range(2)]
        res_bf = [sb(f"res_bf{h}", [P, HALF, PACK], BF16) for h in range(2)]
        res_w = sb("res_w", [P, V], U32)
        res_s = sb("res_s", [P, V], U8)

        def line_up(h, t):
            nc.scalar.activation(sq[h, t], ysq[t][:].indirect(n1_l[:, 16 * h : 16 * (h + 1)]), ACT.Copy)

        def pair_sum(h, t, dst):
            pairs = sq[h, t].rearrange("p (v e) -> p v e", e=2)
            for e in range(2):
                nc.tensor.matmul(dst, pairs[:, :, e], ident[:], is_transpose=True, start=(e == 0), stop=(e == 1))

        def pair_sums(h, tiles, bank):
            ms_ps = psum.tile([P, len(tiles), P], F32, name=f"ms_ps{h}_{tiles[0]}", tag=bank)
            for i, t in enumerate(tiles):
                pair_sum(h, t, ms_ps[:, i, :])
            return tiles, ms_ps

        def finish_z(h, sums):
            root_ps = psum.tile([P, PACK, HALF], F32, name=f"root_ps{h}", tag=f"bank{2 * h + 1}")
            for tiles, ms_ps in sums:
                nc.scalar.activation(root[h][:, tiles[0] : tiles[-1] + 1, :], ms_ps[:], ACT.Sqrt, bias=0.1)
                for t in tiles:
                    nc.tensor.transpose(root_ps[:, t, :], root[h][:, t, :], ident[:])
            nc.vector.tensor_tensor(
                out=z_bf[h][:],
                in0=root_ps[:].rearrange("p t v -> p v t"),
                in1=gs_t[:].unsqueeze(1).to_broadcast([P, HALF, PACK]),
                op=ALU.mult,
            )
            nc.vector.quantize_mx(
                out=z_w[h][:].bitcast(FP8X4), scales=z_s[h][:], in_=z_bf[h][:].rearrange("p v j -> p (v j)")
            )

        def score(h, dst):
            for t in range(PACK):
                nc.tensor.matmul_mx(
                    out=dst[t],
                    lhsT=cand_w[:, P * t : P * (t + 1)].bitcast(FP8X4),
                    lhsT_scale=cand_s[:, P * t : P * (t + 1)],
                    rhs=z_w[h][:].bitcast(FP8X4),
                    rhs_scale=z_s[h][:],
                    start=True,
                    stop=True,
                )

        def fetch(dst, windows, lst, h):
            for t in range(PACK):
                nc.scalar.activation(dst[h][:, t, :], windows[t][:].indirect(lst[:, 8 * h : 8 * (h + 1)]), ACT.Copy)

        sq_first = sb("sq_first", [P, PACK, V], F32)
        sq_mid = sb("sq_mid", [P, 2, V], F32)
        for t in range(PACK):
            sq[0, t] = sq_first[:, t, :]
        for t in range(2):
            sq[1, t] = sq_mid[:, t, :]
        line_up(0, 0)
        for t in range(1, PACK):
            nc.scalar.activation(ysq[t][:], y_ps[t][:], ACT.Square)
            line_up(0, t)
        sums_first = [pair_sums(0, [0, 1, 2, 3], "bank0")]
        for t in range(PACK):
            nc.vector.tensor_scalar(
                out=b_sb[t][:], in0=b_ps[t // 2][:, t % 2, :], scalar1=OUT_SCALE, scalar2=None, op0=ALU.mult
            )
        line_up(1, 0)
        line_up(1, 1)
        finish_z(0, sums_first)
        sq_last = sb("sq_last", [P, 2, V], F32, "sq_first")
        for t in range(2, PACK):
            sq[1, t] = sq_last[:, t - 2, :]
            line_up(1, t)
        sums_last = [pair_sums(1, [0, 1, 2], "bank2"), pair_sums(1, [3], "bank4")]
        score(0, [a_first[:, t, :] for t in range(PACK)])
        finish_z(1, sums_last)
        b_got_all = sb("b_got", [P, 2, PACK, HALF], F32, "sq_first")
        b_got = [b_got_all[:, h] for h in range(2)]
        fetch(b_got, b_sb, n3_l, 0)
        a_last = [psum.tile([P, HALF], F32, name=f"a_last{t}", tag=f"bank{t}") for t in range(PACK)]
        score(1, [tile[:] for tile in a_last])
        first = [sb("first0", [P, PACK, HALF], F32, "z_bf1"), sb("first1", [P, PACK, HALF], F32)]
        for t in range(PACK):
            nc.vector.tensor_copy(out=a_sb[t][:, 0:HALF], in_=a_first[:, t, :])
        nc.vector.tensor_tensor(out=first[0][:], in0=a_first[:], in1=b_got[0], op=ALU.mult)
        fetch(b_got, b_sb, n3_l, 1)
        for t in range(PACK):
            nc.vector.tensor_copy(out=a_sb[t][:, HALF:V], in_=a_last[t][:])
        for t in range(PACK):
            nc.vector.tensor_tensor(out=first[1][:, t, :], in0=a_last[t][:], in1=b_got[1][:, t, :], op=ALU.mult)

        out_rows = out_0.rearrange("(p t) v -> p t v", t=PACK)
        out_words = out_1[0].rearrange("p n t -> p (n t)").bitcast(I32)
        for h in range(2):
            fetch(a_got, a_sb, n2_l, h)
        for h in range(2):
            cols = slice(HALF * h, HALF * (h + 1))
            for u in range(2):
                nc.vector.scalar_tensor_tensor(
                    out=second[h][:, 2 * u : 2 * u + 2, :],
                    in0=b_ps[u][:, :, cols],
                    scalar=OUT_SCALE,
                    in1=a_got[h][:, 2 * u : 2 * u + 2, :],
                    op0=ALU.mult,
                    op1=ALU.mult,
                )
            for u in range(2):
                two = slice(2 * u, 2 * u + 2)
                nc.vector.tensor_tensor(
                    out=res[h][:, two, :], in0=first[h][:, two, :], in1=second[h][:, two, :], op=ALU.subtract
                )
            nc.sync.dma_start(out=out_rows[:, :, cols], in_=res[h][:])
        nc.scalar.copy(out=res_bf[0][:], in_=res[0][:].rearrange("p t v -> p v t"))
        nc.vector.tensor_copy(out=res_bf[1][:], in_=res[1][:].rearrange("p t v -> p v t"))
        for h in range(2):
            cols = slice(HALF * h, HALF * (h + 1))
            nc.vector.quantize_mx(
                out=res_w[:, cols].bitcast(FP8X4), scales=res_s[:, cols], in_=res_bf[h][:].rearrange("p v j -> p (v j)")
            )
            nc.sync.dma_start(out=out_words[:, cols], in_=res_w[:, cols].bitcast(I32))
        scale_rows = out_2[0].bitcast(I32)
        for q in range(4):
            queue = nc.scalar if q % 2 else nc.sync
            queue.dma_start(out=scale_rows[4 * q : 4 * q + 4, :], in_=res_s[32 * q : 32 * q + 4, :].bitcast(I32))
